import numpy as np
import ml_dtypes


def mxq(x, axis, fmt="e4m3"):
    dtype, down = {"e4m3": (ml_dtypes.float8_e4m3fn, 7), "e5m2": (ml_dtypes.float8_e5m2, 14)}[fmt]
    v = np.moveaxis(np.asarray(x, np.float32).astype(ml_dtypes.bfloat16).astype(np.float64), axis, -1)
    blocks = v.reshape(v.shape[:-1] + (-1, 32))
    amax = np.abs(blocks).max(-1, keepdims=True)
    byte = np.maximum(np.where(amax > 0, np.frexp(amax)[1] - 1 + 127, 0) - down, 1)
    scale = np.exp2(byte - 127.0)
    codes = (blocks / scale).astype(np.float32).astype(dtype).astype(np.float64)
    return np.moveaxis((codes * scale).reshape(v.shape), -1, axis)


WIDE = False


def mx_kscale(k):
    if not WIDE:
        return np.ones(k)
    levels = np.array([30, -30])
    if k % 512:
        return np.exp2(np.random.permutation(np.resize(levels, k // 32))).repeat(32)
    a = np.empty((k // 512, 16))
    for p in range(k // 512):
        a[p, :8] = np.random.permutation(np.resize(levels, 8))
        for g in range(8):
            far = levels[np.abs(levels - a[p, g]) >= 10]
            a[p, g + 8] = far[np.random.randint(len(far))]
    return np.exp2(a.ravel()).repeat(32)


def f64(x):
    return np.asarray(x).astype(np.float64)


def striped(idx):
    return np.tile(np.asarray(idx).reshape(-1, 16).T, (8, 1)).astype(np.uint16)


def unstriped(offs):
    return offs[:16].T.reshape(-1).astype(np.int64)


K, J, N, T, S, V = 256, 1024, 256, 2048, 2048, 2048


def setup_inputs():
    n = np.random.standard_normal
    idx = np.random.permutation(T)[:J]
    idx2 = np.random.permutation(S)[:J]
    idx3 = np.random.permutation(V)[:J]
    fj = mx_kscale(J)
    return {
        "xf": (n((K, T))).astype(np.float32),
        "ra": (np.random.uniform(0.5, 1.5, (1, J)) * fj).astype(np.float32),
        "xb": (n((K, S))).astype(np.float32),
        "gt": (n((N, V)) * np.exp(0.5 * n((1, V)))).astype(np.float32),
        "rb": (np.random.uniform(0.5, 1.5, (1, J)) / fj).astype(np.float32),
        "mom": (1.0 * n((K, N))).astype(np.float32),
        "old": (1.0 * n((K, N))).astype(np.float32),
        "offs": striped(idx),
        "offs2": striped(idx2),
        "offs3": striped(idx3),
    }


def reference(xf, ra, xb, gt, rb, mom, old, offs, offs2, offs3):
    idx = unstriped(offs)
    idx2 = unstriped(offs2)
    idx3 = unstriped(offs3)
    us = f64(xf)[:, idx] * f64(xb)[:, idx2] * f64(ra)
    uj = us.T
    gs = f64(gt)[:, idx3] * f64(rb)
    gj = gs.T
    ujq = mxq(uj, 0, "e4m3")
    gjq = mxq(gj, 0, "e5m2")
    w = ujq.T @ gjq
    u2 = 0.04 * w + 0.6 * f64(mom)
    y = f64(old) * 0.5 - u2 / (1.0 + np.abs(u2))
    return y

@@ -1,0 +1,162 @@
+from contextlib import ExitStack
+
+import concourse.mybir as mybir
+from concourse.masks import make_identity
+
+K, J, N, T = 256, 1024, 256, 2048
+FLOPS = 2 * K * J * N
+
+F32 = mybir.dt.float32
+BF16 = mybir.dt.bfloat16
+U32 = mybir.dt.uint32
+U16 = mybir.dt.uint16
+U8 = mybir.dt.uint8
+E4M3 = mybir.dt.float8_e4m3fn_x4
+E5M2 = mybir.dt.float8_e5m2_x4
+ALU = mybir.AluOpType
+ACT = mybir.ActivationFunctionType
+
+P = 128
+PACK = 4
+SLOTS = P * PACK
+PASSES = J // SLOTS
+HALVES = 2
+LIST_ROWS = 16
+VECTOR_SHARE = 256
+
+
+def tile_list_moment_products_listed_momentum_kernel(tc, xf, ra, xb, gt, rb, mom, old, offs, offs2, offs3, out):
+    nc = tc.nc
+    with ExitStack() as ctx:
+        sb = ctx.enter_context(tc.tile_pool(name="sb", bufs=1))
+        turn = ctx.enter_context(tc.psum_pool(name="turn", bufs=6))
+        sums = ctx.enter_context(tc.psum_pool(name="sums", bufs=1))
+
+        def load(name, src, shape, dtype, queue):
+            t = sb.tile(shape, dtype, name=name)
+            queue.dma_start(out=t[:], in_=src)
+            return t
+
+        xf_rows = xf.rearrange("(p h) t -> h p t", h=HALVES)
+        xb_rows = xb.rearrange("(p h) t -> h p t", h=HALVES)
+        gt_rows = gt.rearrange("(h p) t -> h p t", h=HALVES)
+
+        xf0 = load("xf0", xf_rows[0], [P, T], F32, nc.sync)
+        xf_list = load("xf_list", offs, [P, J // LIST_ROWS], U16, nc.sync)
+        xb_list = load("xb_list", offs2, [P, J // LIST_ROWS], U16, nc.sync)
+        xb0 = load("xb0", xb_rows[0], [P, T], F32, nc.sync)
+        ra_col = load("ra_col", ra.rearrange("o (a p t) -> p (o a) t", a=PASSES, t=PACK), [P, PASSES, PACK], F32, nc.sync)
+        gt_list = load("gt_list", offs3, [P, J // LIST_ROWS], U16, nc.sync)
+        gt0 = load("gt0", gt_rows[0], [P, T], F32, nc.sync)
+        rb_col = load("rb_col", rb.rearrange("o (a p t) -> p (o a) t", a=PASSES, t=PACK), [P, PASSES, PACK], F32, nc.sync)
+        gt1 = load("gt1", gt_rows[1], [P, T], F32, nc.sync)
+        xf1 = load("xf1", xf_rows[1], [P, T], F32, nc.sync)
+        xb1 = load("xb1", xb_rows[1], [P, T], F32, nc.sync)
+        mom_sb = load("mom_sb", mom.rearrange("(p h) n -> p h n", h=HALVES), [P, HALVES, N], F32, nc.sync)
+        old_sb = load("old_sb", old.rearrange("(p h) n -> p h n", h=HALVES), [P, HALVES, N], F32, nc.sync)
+        out_rows = out.rearrange("(p h) n -> h p n", h=HALVES)
+
+        ident = sb.tile([P, P], F32, name="ident")
+        make_identity(nc, ident[:])
+
+        def entries(lst, lo, hi):
+            return lst[:, lo // LIST_ROWS : hi // LIST_ROWS]
+
+        def gather(name, table, lst, vector_share):
+            picked = [sb.tile([P, SLOTS], F32, name=name + "_p%d" % a) for a in range(PASSES)]
+            if vector_share:
+                nc.vector.tensor_copy(picked[0][:, :vector_share], table[:].indirect(entries(lst, 0, vector_share)))
+            nc.scalar.activation(picked[0][:, vector_share:], table[:].indirect(entries(lst, vector_share, SLOTS)), ACT.Copy)
+            nc.scalar.activation(picked[1][:], table[:].indirect(entries(lst, SLOTS, J)), ACT.Copy)
+            return picked
+
+        def gather_times(name, table, feat, fused_passes):
+            prod = []
+            for a in range(PASSES):
+                r = sb.tile([P, SLOTS], F32, name=name + "_r%d" % a)
+                lookup = table[:].indirect(entries(xb_list, a * SLOTS, (a + 1) * SLOTS))
+                if a < fused_passes:
+                    nc.vector.tensor_tensor(r[:], lookup, feat[a][:], ALU.mult)
+                else:
+                    picked = sb.tile([P, SLOTS], F32, name=name + "_p%d" % a)
+                    nc.scalar.activation(picked[:], lookup, ACT.Copy)
+                    nc.vector.tensor_tensor(r[:], picked[:], feat[a][:], ALU.mult)
+                prod.append(r)
+            return prod
+
+        def turn_over(name, values, weight):
+            grouped = []
+            for a in range(PASSES):
+                bank = turn.tile([P, PACK, P], F32, name=name + "_bank%d" % a, tag="turn")
+                for t in range(PACK):
+                    nc.tensor.transpose(bank[:, t, :], values[a][:, t:SLOTS:PACK], ident[:])
+                g = sb.tile([P, SLOTS], BF16, name=name + "_g%d" % a, align_bytes=64)
+                nc.vector.tensor_tensor(
+                    g[:].rearrange("p (c t) -> p c t", t=PACK),
+                    bank[:].rearrange("p t c -> p c t"),
+                    weight[:, a : a + 1, :].to_broadcast([P, P, PACK]),
+                    ALU.mult,
+                )
+                grouped.append(g)
+            return grouped
+
+        g_codes = [sb.tile([P, N], U32, name="g_codes%d" % a, align_bytes=64) for a in range(PASSES)]
+        g_scales = [sb.tile([P, N], U8, name="g_scales%d" % a, align_bytes=64) for a in range(PASSES)]
+        u_codes = [[sb.tile([P, P], U32, name="u_codes%d%d" % (h, a), align_bytes=64) for a in range(PASSES)] for h in range(HALVES)]
+        u_scales = [[sb.tile([P, P], U8, name="u_scales%d%d" % (h, a), align_bytes=64) for a in range(PASSES)] for h in range(HALVES)]
+
+        def quantize_g(h, grouped):
+            cols = slice(h * P, (h + 1) * P)
+            for a in range(PASSES):
+                nc.vector.quantize_mx(out=g_codes[a][:, cols].bitcast(E5M2), scales=g_scales[a][:, cols], in_=grouped[a][:])
+
+        def quantize_u(h, grouped):
+            for a in range(PASSES):
+                nc.vector.quantize_mx(out=u_codes[h][a][:].bitcast(E4M3), scales=u_scales[h][a][:], in_=grouped[a][:])
+
+        def moment(h):
+            acc = sums.tile([P, N], F32, name="acc%d" % h)
+            for a in range(PASSES):
+                nc.tensor.matmul_mx(
+                    out=acc[:],
+                    lhsT=u_codes[h][a][:].bitcast(E4M3),
+                    lhsT_scale=u_scales[h][a][:],
+                    rhs=g_codes[a][:].bitcast(E5M2),
+                    rhs_scale=g_scales[a][:],
+                    start=(a == 0),
+                    stop=(a == PASSES - 1),
+                )
+            return acc
+
+        def soften(h, acc):
+            v = sb.tile([P, N], F32, name="v%d" % h)
+            nc.vector.scalar_tensor_tensor(v[:], acc[:], 0.04 / 0.6, mom_sb[:, h, :], ALU.mult, ALU.add)
+            size = sb.tile([P, N], F32, name="size%d" % h)
+            nc.scalar.activation(size[:], v[:], ACT.Abs, scale=0.6)
+            root = sb.tile([P, N], F32, name="root%d" % h)
+            nc.scalar.activation(root[:], size[:], ACT.Abs_reciprocal_sqrt, bias=1.0)
+            inv = sb.tile([P, N], F32, name="inv%d" % h)
+            nc.scalar.activation(inv[:], root[:], ACT.Square)
+            return v, inv
+
+        def finish(h, v, inv):
+            step = sb.tile([P, N], F32, name="step%d" % h)
+            nc.vector.scalar_tensor_tensor(step[:], v[:], -0.6, inv[:], ALU.mult, ALU.mult)
+            res = sb.tile([P, N], F32, name="res%d" % h)
+            nc.vector.scalar_tensor_tensor(res[:], old_sb[:, h, :], 0.5, step[:], ALU.mult, ALU.add)
+            nc.sync.dma_start(out=out_rows[h], in_=res[:])
+
+        feat0 = gather("xf0", xf0, xf_list, 0)
+        quantize_u(0, turn_over("xb0", gather_times("xb0", xb0, feat0, PASSES), ra_col))
+        for h, table in enumerate((gt0, gt1)):
+            name = "gt%d" % h
+            quantize_g(h, turn_over(name, gather(name, table, gt_list, 0), rb_col))
+        feat1 = gather("xf1", xf1, xf_list, VECTOR_SHARE)
+        acc0 = moment(0)
+        grouped1 = turn_over("xb1", gather_times("xb1", xb1, feat1, 1), ra_col)
+        v0, inv0 = soften(0, acc0)
+        quantize_u(1, grouped1)
+        acc1 = moment(1)
+        finish(0, v0, inv0)
+        v1, inv1 = soften(1, acc1)
+        finish(1, v1, inv1)

@@ -22,141 +22,202 @@ SLOTS = P * PACK
 PASSES = J // SLOTS
 HALVES = 2
 LIST_ROWS = 16
-VECTOR_SHARE = 256
+ALIGN = 64
 
 
 def tile_list_moment_products_listed_momentum_kernel(tc, xf, ra, xb, gt, rb, mom, old, offs, offs2, offs3, out):
     nc = tc.nc
     with ExitStack() as ctx:
         sb = ctx.enter_context(tc.tile_pool(name="sb", bufs=1))
-        turn = ctx.enter_context(tc.psum_pool(name="turn", bufs=6))
-        sums = ctx.enter_context(tc.psum_pool(name="sums", bufs=1))
+        ps = ctx.enter_context(tc.psum_pool(name="ps", bufs=1))
+
+        def sbuf(name, width, dtype, on=None):
+            return sb.tile([P, width], dtype, name=name, tag=on or name, align_bytes=ALIGN)
 
         def load(name, src, shape, dtype, queue):
-            t = sb.tile(shape, dtype, name=name)
+            t = sb.tile(shape, dtype, name=name, tag=name, align_bytes=ALIGN)
             queue.dma_start(out=t[:], in_=src)
+            return t
+
+        def load_list(name, src):
+            t = sb.tile([P, J // LIST_ROWS], U16, name=name)
+            nc.sync.dma_start(out=t[:], in_=src)
             return t
 
         xf_rows = xf.rearrange("(p h) t -> h p t", h=HALVES)
         xb_rows = xb.rearrange("(p h) t -> h p t", h=HALVES)
         gt_rows = gt.rearrange("(h p) t -> h p t", h=HALVES)
+        out_rows = out.rearrange("(p h) n -> h p n", h=HALVES)
 
-        xf0 = load("xf0", xf_rows[0], [P, T], F32, nc.sync)
-        xf_list = load("xf_list", offs, [P, J // LIST_ROWS], U16, nc.sync)
-        xb_list = load("xb_list", offs2, [P, J // LIST_ROWS], U16, nc.sync)
-        xb0 = load("xb0", xb_rows[0], [P, T], F32, nc.sync)
-        ra_col = load("ra_col", ra.rearrange("o (a p t) -> p (o a) t", a=PASSES, t=PACK), [P, PASSES, PACK], F32, nc.sync)
-        gt_list = load("gt_list", offs3, [P, J // LIST_ROWS], U16, nc.sync)
+        def load_weights(name, src):
+            t = sb.tile([P, PASSES, 2 * PACK], F32, name=name)
+            nc.sync.dma_start(out=t[:, :, :PACK], in_=src.rearrange("o (a p t) -> p (o a) t", a=PASSES, t=PACK))
+            return t
+
+        rb_col = load_weights("rb_col", rb)
+        ra_col = load_weights("ra_col", ra)
         gt0 = load("gt0", gt_rows[0], [P, T], F32, nc.sync)
-        rb_col = load("rb_col", rb.rearrange("o (a p t) -> p (o a) t", a=PASSES, t=PACK), [P, PASSES, PACK], F32, nc.sync)
+        gt_list = load_list("gt_list", offs3)
         gt1 = load("gt1", gt_rows[1], [P, T], F32, nc.sync)
+        xf_list = load_list("xf_list", offs)
+        xf0 = load("xf0", xf_rows[0], [P, T], F32, nc.sync)
+        xb_list = load_list("xb_list", offs2)
+        xb0 = load("xb0", xb_rows[0], [P, T], F32, nc.sync)
         xf1 = load("xf1", xf_rows[1], [P, T], F32, nc.sync)
         xb1 = load("xb1", xb_rows[1], [P, T], F32, nc.sync)
         mom_sb = load("mom_sb", mom.rearrange("(p h) n -> p h n", h=HALVES), [P, HALVES, N], F32, nc.sync)
         old_sb = load("old_sb", old.rearrange("(p h) n -> p h n", h=HALVES), [P, HALVES, N], F32, nc.sync)
-        out_rows = out.rearrange("(p h) n -> h p n", h=HALVES)
 
-        ident = sb.tile([P, P], F32, name="ident")
+        warm_in = sbuf("warm_in", 1, F32)
+        nc.vector.memset(warm_in[:], 1.0)
+        warm_out = sbuf("warm_out", 1, F32)
+        nc.scalar.activation(warm_out[:], warm_in[:], ACT.Abs_reciprocal_sqrt, bias=1.0)
+
+        ident = sbuf("ident", P, F32)
         make_identity(nc, ident[:])
+
+        def spread(name, col, a, bank_tag):
+            bank = ps.tile([P, PACK, P], F32, name=name + "_bank", tag=bank_tag)
+            for t in range(PACK):
+                nc.tensor.transpose(bank[:, t, :], col[:, a, t : t + 1].to_broadcast([P, P]), ident[:])
+            return bank[:].rearrange("p t q -> p q t")
+
+        def by_four(ap):
+            return ap.rearrange("p (q t) -> p q t", t=PACK)
+
+        ra_rows = [spread("ra0", ra_col, 0, "bank2")]
+        rb_rows = [spread("rb%d" % a, rb_col, a, ("bank0", "bank1")[a]) for a in range(PASSES)]
+        ra_rows.append(spread("ra1", ra_col, 1, "bank3"))
+        ra_first = sbuf("ra_first", SLOTS, F32)
+        nc.scalar.copy(out=by_four(ra_first[:]), in_=ra_rows[0])
 
         def entries(lst, lo, hi):
             return lst[:, lo // LIST_ROWS : hi // LIST_ROWS]
 
-        def gather(name, table, lst, vector_share):
-            picked = [sb.tile([P, SLOTS], F32, name=name + "_p%d" % a) for a in range(PASSES)]
-            if vector_share:
-                nc.vector.tensor_copy(picked[0][:, :vector_share], table[:].indirect(entries(lst, 0, vector_share)))
-            nc.scalar.activation(picked[0][:, vector_share:], table[:].indirect(entries(lst, vector_share, SLOTS)), ACT.Copy)
-            nc.scalar.activation(picked[1][:], table[:].indirect(entries(lst, SLOTS, J)), ACT.Copy)
-            return picked
+        def weighted_features(name, table, first_on, picked_on):
+            first = sbuf(name + "_w0", SLOTS, F32, first_on)
+            nc.vector.tensor_tensor(first[:], table[:].indirect(entries(xf_list, 0, SLOTS)), ra_first[:], ALU.mult)
+            picked = sbuf(name + "_p1", SLOTS, F32, picked_on)
+            nc.scalar.activation(picked[:], table[:].indirect(entries(xf_list, SLOTS, J)), ACT.Copy)
+            second = sbuf(name + "_w1", SLOTS, F32)
+            nc.vector.tensor_tensor(by_four(second[:]), by_four(picked[:]), ra_rows[1], ALU.mult)
+            return [by_four(first[:]), by_four(second[:])]
 
-        def gather_times(name, table, feat, fused_passes):
-            prod = []
-            for a in range(PASSES):
-                r = sb.tile([P, SLOTS], F32, name=name + "_r%d" % a)
-                lookup = table[:].indirect(entries(xb_list, a * SLOTS, (a + 1) * SLOTS))
-                if a < fused_passes:
-                    nc.vector.tensor_tensor(r[:], lookup, feat[a][:], ALU.mult)
-                else:
-                    picked = sb.tile([P, SLOTS], F32, name=name + "_p%d" % a)
-                    nc.scalar.activation(picked[:], lookup, ACT.Copy)
-                    nc.vector.tensor_tensor(r[:], picked[:], feat[a][:], ALU.mult)
-                prod.append(r)
-            return prod
+        def gather(name, table, lst, share, vector_on=None, scalar_on=None):
+            by_scalar = sbuf(name + "_s", J - share, F32, scalar_on)
+            by_vector = sbuf(name + "_v", share, F32, vector_on)
+            nc.vector.tensor_copy(by_vector[:], table[:].indirect(entries(lst, 0, share)))
+            pieces = []
+            for lo, hi in ((share, SLOTS), (SLOTS, J)):
+                piece = by_scalar[:, lo - share : hi - share]
+                nc.scalar.activation(piece, table[:].indirect(entries(lst, lo, hi)), ACT.Copy)
+                pieces.append((lo, hi, piece))
+            return [pieces[0], (0, share, by_vector[:]), pieces[1]]
 
-        def turn_over(name, values, weight):
-            grouped = []
-            for a in range(PASSES):
-                bank = turn.tile([P, PACK, P], F32, name=name + "_bank%d" % a, tag="turn")
-                for t in range(PACK):
-                    nc.tensor.transpose(bank[:, t, :], values[a][:, t:SLOTS:PACK], ident[:])
-                g = sb.tile([P, SLOTS], BF16, name=name + "_g%d" % a, align_bytes=64)
-                nc.vector.tensor_tensor(
-                    g[:].rearrange("p (c t) -> p c t", t=PACK),
-                    bank[:].rearrange("p t c -> p c t"),
-                    weight[:, a : a + 1, :].to_broadcast([P, P, PACK]),
-                    ALU.mult,
-                )
-                grouped.append(g)
+        def multiply(name, pieces, factors):
+            rounded = [sbuf(name + "_r%d" % a, SLOTS, BF16) for a in range(PASSES)]
+            for lo, hi, piece in pieces:
+                a, first = divmod(lo, SLOTS)
+                quads = slice(first // PACK, (first + hi - lo) // PACK)
+                nc.vector.tensor_tensor(by_four(rounded[a][:])[:, quads, :], by_four(piece), factors[a][:, quads, :], ALU.mult)
+            return rounded
+
+        def turn(name, rounded, bank_tag):
+            bank = ps.tile([P, len(rounded), 2, P], F32, name=name + "_bank", tag=bank_tag)
+            for a, r in enumerate(rounded):
+                words = r[:].bitcast(F32)
+                for u in range(2):
+                    nc.tensor.transpose(bank[:, a, u, :], words[:, u : 2 * P : 2], ident[:])
+            return bank
+
+        def weave(name, bank, on=None):
+            passes = bank.shape[1]
+            grouped = sbuf(name + "_g", passes * SLOTS, BF16, on)
+            nc.scalar.copy(
+                out=grouped[:].bitcast(F32).rearrange("p (a c u) -> p a c u", a=passes, u=2),
+                in_=bank[:].rearrange("p a u c -> p a c u"),
+            )
             return grouped
 
-        g_codes = [sb.tile([P, N], U32, name="g_codes%d" % a, align_bytes=64) for a in range(PASSES)]
-        g_scales = [sb.tile([P, N], U8, name="g_scales%d" % a, align_bytes=64) for a in range(PASSES)]
-        u_codes = [[sb.tile([P, P], U32, name="u_codes%d%d" % (h, a), align_bytes=64) for a in range(PASSES)] for h in range(HALVES)]
-        u_scales = [[sb.tile([P, P], U8, name="u_scales%d%d" % (h, a), align_bytes=64) for a in range(PASSES)] for h in range(HALVES)]
+        def quantize(name, grouped, fmt, on=None):
+            width = grouped.shape[1] // PACK
+            codes = sbuf(name + "_codes", width, U32)
+            scales = sbuf(name + "_scales", width, U8, on)
+            nc.vector.quantize_mx(out=codes[:].bitcast(fmt), scales=scales[:], in_=grouped[:])
+            return [(codes[:, c : c + P].bitcast(fmt), scales[:, c : c + P]) for c in range(0, width, P)]
 
-        def quantize_g(h, grouped):
-            cols = slice(h * P, (h + 1) * P)
+        def multiply_mx(acc, u_pass, g_pass, a):
+            nc.tensor.matmul_mx(
+                out=acc,
+                lhsT=u_pass[0],
+                lhsT_scale=u_pass[1],
+                rhs=g_pass[0],
+                rhs_scale=g_pass[1],
+                start=(a == 0),
+                stop=(a == PASSES - 1),
+            )
+
+        def join(h, accs, on=None):
+            vs = []
+            for i, acc in enumerate(accs):
+                width = acc.shape[1]
+                v = sbuf("v%d%d" % (h, i), width, F32, on)
+                nc.vector.scalar_tensor_tensor(v[:], acc[:], 0.04 / 0.6, mom_sb[:, h, i * width : (i + 1) * width], ALU.mult, ALU.add)
+                vs.append(v)
+            return vs
+
+        def soften(h, vs, on=None):
+            sizes = [sbuf("size%d%d" % (h, i), v.shape[1], F32, on) for i, v in enumerate(vs)]
+            roots = [sbuf("root%d%d" % (h, i), v.shape[1], F32) for i, v in enumerate(vs)]
+            invs = [sbuf("inv%d%d" % (h, i), v.shape[1], F32) for i, v in enumerate(vs)]
+            for size, v in zip(sizes, vs):
+                nc.scalar.activation(size[:], v[:], ACT.Abs, scale=0.6)
+            for root, size in zip(roots, sizes):
+                nc.scalar.activation(root[:], size[:], ACT.Abs_reciprocal_sqrt, bias=1.0)
+            for inv, root in zip(invs, roots):
+                nc.scalar.activation(inv[:], root[:], ACT.Square)
+            return invs
+
+        def finish(h, vs, invs, on=None):
+            steps = [sbuf("step%d%d" % (h, i), v.shape[1], F32, on) for i, v in enumerate(vs)]
+            for step, v, inv in zip(steps, vs, invs):
+                nc.vector.scalar_tensor_tensor(step[:], v[:], -0.6, inv[:], ALU.mult, ALU.mult)
+            for i, step in enumerate(steps):
+                width = step.shape[1]
+                cols = slice(i * width, (i + 1) * width)
+                res = sbuf("res%d%d" % (h, i), width, F32)
+                nc.vector.scalar_tensor_tensor(res[:], old_sb[:, h, cols], 0.5, step[:], ALU.mult, ALU.add)
+                nc.sync.dma_start(out=out_rows[h][:, cols], in_=res[:])
+
+        g0_bank = turn("g0", multiply("gt0", gather("gt0", gt0, gt_list, 384, "slot_a", "slot_b"), rb_rows), "bank4")
+        g1_bank = turn("g1", multiply("gt1", gather("gt1", gt1, gt_list, 384, "slot_b", "slot_a"), rb_rows), "bank5")
+        g0_grouped = weave("g0", g0_bank, on="gt1")
+
+        feat0 = weighted_features("xf0", xf0, None, None)
+        g_mx = [quantize("g0", g0_grouped, E5M2, on="xf0")]
+
+        u0_bank = turn("u0", multiply("xb0", gather("xb0", xb0, xb_list, 384), feat0), "bank6")
+        g1_grouped = weave("g1", g1_bank, on="xb0")
+
+        feat1 = weighted_features("xf1", xf1, None, None)
+        g_mx.append(quantize("g1", g1_grouped, E5M2, on="ra_first"))
+        u0_mx = quantize("u0", weave("u0", u0_bank, on="xf1"), E4M3)
+        acc0 = ps.tile([P, N], F32, name="acc0", tag="bank2")
+        for half in range(HALVES):
             for a in range(PASSES):
-                nc.vector.quantize_mx(out=g_codes[a][:, cols].bitcast(E5M2), scales=g_scales[a][:, cols], in_=grouped[a][:])
+                multiply_mx(acc0[:, half * P : (half + 1) * P], u0_mx[a], g_mx[half][a], a)
 
-        def quantize_u(h, grouped):
-            for a in range(PASSES):
-                nc.vector.quantize_mx(out=u_codes[h][a][:].bitcast(E4M3), scales=u_scales[h][a][:], in_=grouped[a][:])
+        rounded1 = multiply("xb1", gather("xb1", xb1, xb_list, 320), feat1)
+        grouped1 = [weave("u1%d" % a, turn("u1%d" % a, rounded1[a : a + 1], ("bank4", "bank5")[a])) for a in range(PASSES)]
 
-        def moment(h):
-            acc = sums.tile([P, N], F32, name="acc%d" % h)
-            for a in range(PASSES):
-                nc.tensor.matmul_mx(
-                    out=acc[:],
-                    lhsT=u_codes[h][a][:].bitcast(E4M3),
-                    lhsT_scale=u_scales[h][a][:],
-                    rhs=g_codes[a][:].bitcast(E5M2),
-                    rhs_scale=g_scales[a][:],
-                    start=(a == 0),
-                    stop=(a == PASSES - 1),
-                )
-            return acc
-
-        def soften(h, acc):
-            v = sb.tile([P, N], F32, name="v%d" % h)
-            nc.vector.scalar_tensor_tensor(v[:], acc[:], 0.04 / 0.6, mom_sb[:, h, :], ALU.mult, ALU.add)
-            size = sb.tile([P, N], F32, name="size%d" % h)
-            nc.scalar.activation(size[:], v[:], ACT.Abs, scale=0.6)
-            root = sb.tile([P, N], F32, name="root%d" % h)
-            nc.scalar.activation(root[:], size[:], ACT.Abs_reciprocal_sqrt, bias=1.0)
-            inv = sb.tile([P, N], F32, name="inv%d" % h)
-            nc.scalar.activation(inv[:], root[:], ACT.Square)
-            return v, inv
-
-        def finish(h, v, inv):
-            step = sb.tile([P, N], F32, name="step%d" % h)
-            nc.vector.scalar_tensor_tensor(step[:], v[:], -0.6, inv[:], ALU.mult, ALU.mult)
-            res = sb.tile([P, N], F32, name="res%d" % h)
-            nc.vector.scalar_tensor_tensor(res[:], old_sb[:, h, :], 0.5, step[:], ALU.mult, ALU.add)
-            nc.sync.dma_start(out=out_rows[h], in_=res[:])
-
-        feat0 = gather("xf0", xf0, xf_list, 0)
-        quantize_u(0, turn_over("xb0", gather_times("xb0", xb0, feat0, PASSES), ra_col))
-        for h, table in enumerate((gt0, gt1)):
-            name = "gt%d" % h
-            quantize_g(h, turn_over(name, gather(name, table, gt_list, 0), rb_col))
-        feat1 = gather("xf1", xf1, xf_list, VECTOR_SHARE)
-        acc0 = moment(0)
-        grouped1 = turn_over("xb1", gather_times("xb1", xb1, feat1, 1), ra_col)
-        v0, inv0 = soften(0, acc0)
-        quantize_u(1, grouped1)
-        acc1 = moment(1)
-        finish(0, v0, inv0)
-        v1, inv1 = soften(1, acc1)
+        v0 = join(0, [acc0], on="xb1_s")
+        u1_mx = [quantize("u1%d" % a, grouped1[a], E4M3)[0] for a in range(PASSES)]
+        inv0 = soften(0, v0, on="xb1_r1")
+        acc1 = [ps.tile([P, P], F32, name="acc1%d" % half, tag=("bank0", "bank1")[half]) for half in range(HALVES)]
+        for a in range(PASSES):
+            for half in range(HALVES):
+                multiply_mx(acc1[half][:], u1_mx[a], g_mx[half][a], a)
+        v1 = join(1, acc1)
+        inv1 = soften(1, v1)
+        finish(0, v0, inv0, on="u11_g")
         finish(1, v1, inv1)

from contextlib import ExitStack

import concourse.mybir as mybir
from concourse.masks import make_identity

K, J, N, T = 256, 1024, 256, 2048
FLOPS = 2 * K * J * N

F32 = mybir.dt.float32
BF16 = mybir.dt.bfloat16
U32 = mybir.dt.uint32
U16 = mybir.dt.uint16
U8 = mybir.dt.uint8
E4M3 = mybir.dt.float8_e4m3fn_x4
E5M2 = mybir.dt.float8_e5m2_x4
ALU = mybir.AluOpType
ACT = mybir.ActivationFunctionType

P = 128
PACK = 4
SLOTS = P * PACK
PASSES = J // SLOTS
HALVES = 2
LIST_ROWS = 16
ALIGN = 64


def tile_list_moment_products_listed_momentum_kernel(tc, xf, ra, xb, gt, rb, mom, old, offs, offs2, offs3, out):
    nc = tc.nc
    with ExitStack() as ctx:
        sb = ctx.enter_context(tc.tile_pool(name="sb", bufs=1))
        ps = ctx.enter_context(tc.psum_pool(name="ps", bufs=1))

        def sbuf(name, width, dtype, on=None):
            return sb.tile([P, width], dtype, name=name, tag=on or name, align_bytes=ALIGN)

        def load(name, src, shape, dtype, queue):
            t = sb.tile(shape, dtype, name=name, tag=name, align_bytes=ALIGN)
            queue.dma_start(out=t[:], in_=src)
            return t

        def load_list(name, src):
            t = sb.tile([P, J // LIST_ROWS], U16, name=name)
            nc.sync.dma_start(out=t[:], in_=src)
            return t

        xf_rows = xf.rearrange("(p h) t -> h p t", h=HALVES)
        xb_rows = xb.rearrange("(p h) t -> h p t", h=HALVES)
        gt_rows = gt.rearrange("(h p) t -> h p t", h=HALVES)
        out_rows = out.rearrange("(p h) n -> h p n", h=HALVES)

        def load_weights(name, src):
            t = sb.tile([P, PASSES, 2 * PACK], F32, name=name)
            nc.sync.dma_start(out=t[:, :, :PACK], in_=src.rearrange("o (a p t) -> p (o a) t", a=PASSES, t=PACK))
            return t

        rb_col = load_weights("rb_col", rb)
        ra_col = load_weights("ra_col", ra)
        gt0 = load("gt0", gt_rows[0], [P, T], F32, nc.sync)
        gt_list = load_list("gt_list", offs3)
        gt1 = load("gt1", gt_rows[1], [P, T], F32, nc.sync)
        xf_list = load_list("xf_list", offs)
        xf0 = load("xf0", xf_rows[0], [P, T], F32, nc.sync)
        xb_list = load_list("xb_list", offs2)
        xb0 = load("xb0", xb_rows[0], [P, T], F32, nc.sync)
        xf1 = load("xf1", xf_rows[1], [P, T], F32, nc.sync)
        xb1 = load("xb1", xb_rows[1], [P, T], F32, nc.sync)
        mom_sb = load("mom_sb", mom.rearrange("(p h) n -> p h n", h=HALVES), [P, HALVES, N], F32, nc.sync)
        old_sb = load("old_sb", old.rearrange("(p h) n -> p h n", h=HALVES), [P, HALVES, N], F32, nc.sync)

        warm_in = sbuf("warm_in", 1, F32)
        nc.vector.memset(warm_in[:], 1.0)
        warm_out = sbuf("warm_out", 1, F32)
        nc.scalar.activation(warm_out[:], warm_in[:], ACT.Abs_reciprocal_sqrt, bias=1.0)

        ident = sbuf("ident", P, F32)
        make_identity(nc, ident[:])

        def spread(name, col, a, bank_tag):
            bank = ps.tile([P, PACK, P], F32, name=name + "_bank", tag=bank_tag)
            for t in range(PACK):
                nc.tensor.transpose(bank[:, t, :], col[:, a, t : t + 1].to_broadcast([P, P]), ident[:])
            return bank[:].rearrange("p t q -> p q t")

        def by_four(ap):
            return ap.rearrange("p (q t) -> p q t", t=PACK)

        ra_rows = [spread("ra0", ra_col, 0, "bank2")]
        rb_rows = [spread("rb%d" % a, rb_col, a, ("bank0", "bank1")[a]) for a in range(PASSES)]
        ra_rows.append(spread("ra1", ra_col, 1, "bank3"))
        ra_first = sbuf("ra_first", SLOTS, F32)
        nc.scalar.copy(out=by_four(ra_first[:]), in_=ra_rows[0])

        def entries(lst, lo, hi):
            return lst[:, lo // LIST_ROWS : hi // LIST_ROWS]

        def weighted_features(name, table, first_on, picked_on):
            first = sbuf(name + "_w0", SLOTS, F32, first_on)
            nc.vector.tensor_tensor(first[:], table[:].indirect(entries(xf_list, 0, SLOTS)), ra_first[:], ALU.mult)
            picked = sbuf(name + "_p1", SLOTS, F32, picked_on)
            nc.scalar.activation(picked[:], table[:].indirect(entries(xf_list, SLOTS, J)), ACT.Copy)
            second = sbuf(name + "_w1", SLOTS, F32)
            nc.vector.tensor_tensor(by_four(second[:]), by_four(picked[:]), ra_rows[1], ALU.mult)
            return [by_four(first[:]), by_four(second[:])]

        def gather(name, table, lst, share, vector_on=None, scalar_on=None):
            by_scalar = sbuf(name + "_s", J - share, F32, scalar_on)
            by_vector = sbuf(name + "_v", share, F32, vector_on)
            nc.vector.tensor_copy(by_vector[:], table[:].indirect(entries(lst, 0, share)))
            pieces = []
            for lo, hi in ((share, SLOTS), (SLOTS, J)):
                piece = by_scalar[:, lo - share : hi - share]
                nc.scalar.activation(piece, table[:].indirect(entries(lst, lo, hi)), ACT.Copy)
                pieces.append((lo, hi, piece))
            return [pieces[0], (0, share, by_vector[:]), pieces[1]]

        def multiply(name, pieces, factors):
            rounded = [sbuf(name + "_r%d" % a, SLOTS, BF16) for a in range(PASSES)]
            for lo, hi, piece in pieces:
                a, first = divmod(lo, SLOTS)
                quads = slice(first // PACK, (first + hi - lo) // PACK)
                nc.vector.tensor_tensor(by_four(rounded[a][:])[:, quads, :], by_four(piece), factors[a][:, quads, :], ALU.mult)
            return rounded

        def turn(name, rounded, bank_tag):
            bank = ps.tile([P, len(rounded), 2, P], F32, name=name + "_bank", tag=bank_tag)
            for a, r in enumerate(rounded):
                words = r[:].bitcast(F32)
                for u in range(2):
                    nc.tensor.transpose(bank[:, a, u, :], words[:, u : 2 * P : 2], ident[:])
            return bank

        def weave(name, bank, on=None):
            passes = bank.shape[1]
            grouped = sbuf(name + "_g", passes * SLOTS, BF16, on)
            nc.scalar.copy(
                out=grouped[:].bitcast(F32).rearrange("p (a c u) -> p a c u", a=passes, u=2),
                in_=bank[:].rearrange("p a u c -> p a c u"),
            )
            return grouped

        def quantize(name, grouped, fmt, on=None):
            width = grouped.shape[1] // PACK
            codes = sbuf(name + "_codes", width, U32)
            scales = sbuf(name + "_scales", width, U8, on)
            nc.vector.quantize_mx(out=codes[:].bitcast(fmt), scales=scales[:], in_=grouped[:])
            return [(codes[:, c : c + P].bitcast(fmt), scales[:, c : c + P]) for c in range(0, width, P)]

        def multiply_mx(acc, u_pass, g_pass, a):
            nc.tensor.matmul_mx(
                out=acc,
                lhsT=u_pass[0],
                lhsT_scale=u_pass[1],
                rhs=g_pass[0],
                rhs_scale=g_pass[1],
                start=(a == 0),
                stop=(a == PASSES - 1),
            )

        def join(h, accs, on=None):
            vs = []
            for i, acc in enumerate(accs):
                width = acc.shape[1]
                v = sbuf("v%d%d" % (h, i), width, F32, on)
                nc.vector.scalar_tensor_tensor(v[:], acc[:], 0.04 / 0.6, mom_sb[:, h, i * width : (i + 1) * width], ALU.mult, ALU.add)
                vs.append(v)
            return vs

        def soften(h, vs, on=None):
            sizes = [sbuf("size%d%d" % (h, i), v.shape[1], F32, on) for i, v in enumerate(vs)]
            roots = [sbuf("root%d%d" % (h, i), v.shape[1], F32) for i, v in enumerate(vs)]
            invs = [sbuf("inv%d%d" % (h, i), v.shape[1], F32) for i, v in enumerate(vs)]
            for size, v in zip(sizes, vs):
                nc.scalar.activation(size[:], v[:], ACT.Abs, scale=0.6)
            for root, size in zip(roots, sizes):
                nc.scalar.activation(root[:], size[:], ACT.Abs_reciprocal_sqrt, bias=1.0)
            for inv, root in zip(invs, roots):
                nc.scalar.activation(inv[:], root[:], ACT.Square)
            return invs

        def finish(h, vs, invs, on=None):
            steps = [sbuf("step%d%d" % (h, i), v.shape[1], F32, on) for i, v in enumerate(vs)]
            for step, v, inv in zip(steps, vs, invs):
                nc.vector.scalar_tensor_tensor(step[:], v[:], -0.6, inv[:], ALU.mult, ALU.mult)
            for i, step in enumerate(steps):
                width = step.shape[1]
                cols = slice(i * width, (i + 1) * width)
                res = sbuf("res%d%d" % (h, i), width, F32)
                nc.vector.scalar_tensor_tensor(res[:], old_sb[:, h, cols], 0.5, step[:], ALU.mult, ALU.add)
                nc.sync.dma_start(out=out_rows[h][:, cols], in_=res[:])

        g0_bank = turn("g0", multiply("gt0", gather("gt0", gt0, gt_list, 384, "slot_a", "slot_b"), rb_rows), "bank4")
        g1_bank = turn("g1", multiply("gt1", gather("gt1", gt1, gt_list, 384, "slot_b", "slot_a"), rb_rows), "bank5")
        g0_grouped = weave("g0", g0_bank, on="gt1")

        feat0 = weighted_features("xf0", xf0, None, None)
        g_mx = [quantize("g0", g0_grouped, E5M2, on="xf0")]

        u0_bank = turn("u0", multiply("xb0", gather("xb0", xb0, xb_list, 384), feat0), "bank6")
        g1_grouped = weave("g1", g1_bank, on="xb0")

        feat1 = weighted_features("xf1", xf1, None, None)
        g_mx.append(quantize("g1", g1_grouped, E5M2, on="ra_first"))
        u0_mx = quantize("u0", weave("u0", u0_bank, on="xf1"), E4M3)
        acc0 = ps.tile([P, N], F32, name="acc0", tag="bank2")
        for half in range(HALVES):
            for a in range(PASSES):
                multiply_mx(acc0[:, half * P : (half + 1) * P], u0_mx[a], g_mx[half][a], a)

        rounded1 = multiply("xb1", gather("xb1", xb1, xb_list, 320), feat1)
        grouped1 = [weave("u1%d" % a, turn("u1%d" % a, rounded1[a : a + 1], ("bank4", "bank5")[a])) for a in range(PASSES)]

        v0 = join(0, [acc0], on="xb1_s")
        u1_mx = [quantize("u1%d" % a, grouped1[a], E4M3)[0] for a in range(PASSES)]
        inv0 = soften(0, v0, on="xb1_r1")
        acc1 = [ps.tile([P, P], F32, name="acc1%d" % half, tag=("bank0", "bank1")[half]) for half in range(HALVES)]
        for a in range(PASSES):
            for half in range(HALVES):
                multiply_mx(acc1[half][:], u1_mx[a], g_mx[half][a], a)
        v1 = join(1, acc1)
        inv1 = soften(1, v1)
        finish(0, v0, inv0, on="u11_g")
        finish(1, v1, inv1)
